import numpy as np, ml_dtypes
CORES = [19,147,275,403]
N = 4
import mx_ref
NC, G, GR = 128, 2, 2
C = np.float32(0.029)
BF = ml_dtypes.bfloat16
def cut(t, i, w=512):
    return t[:, w * i:w * i + w]
def tile(rs):
    return np.stack(rs, axis=2).reshape(128, -1).astype(BF)
def layer(w, X):
    out = []
    for i in range(G):
        for t in range(len(X)):
            p = mx_ref.matmul(mx_ref.quantize(cut(w, len(X) * i + t)), X[t])
            z = p if t == 0 else z + p
        out.append(z)
    return out
def act(Z):
    return [np.maximum(s * z, 0) * C for z in Z for s in (1, -1)]
def setup_inputs(rng):
    def f(*shape):
        return mx_ref.flush((rng.standard_normal(shape, dtype=np.float32) * np.exp2(rng.integers(-2, 3, shape[:-1] + (1,)))).astype(BF))
    return {"xa": f(N, 128, 512), "xb": f(N, 128, 4 * NC), "wa": f(N, 128, G * 512), "wb": f(N, 128, G * 512)}
def setup_inputs_blocks(rng):
    d = setup_inputs(rng)
    for k in ("xa", "xb", "wa", "wb"): d[k] = mx_ref.spread(d[k], rng, 2)
    return d
def setup_inputs_wide(rng):
    d = setup_inputs(rng)
    for k in ("xa", "xb", "wa", "wb"): d[k] = mx_ref.flush((d[k].astype(np.float32) * np.exp2(rng.integers(-5, 6, (N, 1, 1))).astype(np.float32)).astype(BF))
    return d
def reference(xa, xb, wa, wb):
    A = [mx_ref.quantize(tile(act(layer(wa[j], [mx_ref.quantize(xa[j])])))) for j in range(N)]
    M = [mx_ref.quantize(tile(act(layer(wb[j], [mx_ref.quantize(xb[j])])))) for j in range(N)]
    y = np.zeros((N, 128, NC), np.float32)
    for r in range(N):
        i, j = divmod(r, GR)
        for k in range(GR):
            p = mx_ref.matmul(A[GR * i + k], M[GR * k + j])
            y[r] = p if k == 0 else y[r] + p
    return {"y": y}

@@ -1,0 +1,142 @@
+from concourse.mybir import dt, AluOpType, ActivationFunctionType
+
+NC = 128
+TW = 4 * NC
+GR = 2
+SCALE = 0.029
+
+_C, _S = "float8_e4m3fn_x4", "uint8"
+SCRATCH = {
+    "t_xb": ("sbuf", [128, TW], "bfloat16"), "t_wb": ("sbuf", [128, 2 * TW], "bfloat16"),
+    "t_xa": ("sbuf", [128, TW], "bfloat16"), "t_wa": ("sbuf", [128, 2 * TW], "bfloat16"),
+    "t_a": ("sbuf", [128, TW], "bfloat16"), "t_b": ("sbuf", [128, TW], "bfloat16"),
+    "c_xb": ("sbuf", [128, NC], _C), "s_xb": ("sbuf", [128, NC], _S),
+    "c_wb": ("sbuf", [128, 2 * NC], _C), "s_wb": ("sbuf", [128, 2 * NC], _S),
+    "c_xa": ("sbuf", [128, NC], _C), "s_xa": ("sbuf", [128, NC], _S),
+    "c_wa": ("sbuf", [128, 2 * NC], _C), "s_wa": ("sbuf", [128, 2 * NC], _S),
+    "c_a": ("sbuf", [128, NC], _C), "s_a": ("sbuf", [128, NC], _S),
+    "c_b": ("sbuf", [128, NC], _C), "s_b": ("sbuf", [128, NC], _S),
+    "r_ac": ("sbuf", [128, NC], _C), "r_as": ("sbuf", [128, NC], _S),
+    "r_bc": ("sbuf", [128, NC], _C), "r_bs": ("sbuf", [128, NC], _S),
+    "h_c": ("sbuf", [128, NC], _C), "h_s": ("sbuf", [128, NC], _S),
+    "o": ("sbuf", [128, NC], "float32"),
+    "zb0": ("psum", [128, 512], "float32"), "zb1": ("psum", [128, 512], "float32"),
+    "za0": ("psum", [128, 512], "float32"), "za1": ("psum", [128, 512], "float32"),
+    "zy": ("psum", [128, 512], "float32"),
+}
+SEMAPHORES = ["out", "arr_hc", "arr_hs", "arr_ac", "arr_as", "arr_bc", "arr_bs", "fin", "stored", "y_mm"]
+for _t in ("a", "b"):
+    SEMAPHORES += [_n + _t for _n in ("l_x", "l_w0", "l_w1", "q_x", "q_w0", "q_w1", "m0", "m1", "act", "vec", "q_t")]
+
+
+def _helpers(src, dst, topo):
+    host = topo.host(src)
+    free = [c for c in range(512)
+            if topo.chip(c) == topo.chip(src) and topo.die(c) != topo.die(src)
+            and topo.may_write(src, c) and topo.may_write(c, dst) and topo.host(c) not in (host, topo.host(dst))]
+    far = [c for c in free if topo.rack(topo.host(c)) != topo.rack(host)]
+    near = [c for c in free if topo.rack(topo.host(c)) == topo.rack(host)]
+    return far[0], near[-1]
+
+
+def _engines(src, dst, topo):
+    bits = [e for e in range(16) if topo.mask(src, dst) >> e & 1]
+    return sum(1 << e for e in bits[::2]), len(bits[::2])
+
+
+def rank_program(g, core, T, topo):
+    cores = list(T.cores)
+    partner_b = {c: cores[(r + GR) % len(cores)] for r, c in enumerate(cores)}
+    rank = T.rank_of(core)
+    sem = T.sem
+    u8 = dt.uint8
+
+    def send(dst, out_ap, in_ap, remote_sem):
+        rid, pid = topo.addr(dst, core)
+        m, n = _engines(core, dst, topo)
+        g.remote_dma(out_ap=out_ap, in_ap=in_ap, remote_sem=remote_sem, local_sem=sem.out, pid=pid, routing_id=rid,
+                     dma_engine_mask=m)
+        return n
+
+    if rank is None:
+        for src in cores:
+            dst = partner_b[src]
+            hc, hs = _helpers(src, dst, topo)
+            if core == hc:
+                g.wait_ge(sem.arr_hc, _engines(src, core, topo)[1])
+                n = send(dst, T.r_bc[:, 0:NC].bitcast(u8), T.h_c[:, 0:NC].bitcast(u8), sem.arr_bc)
+                g.wait_ge(sem.out, n)
+            elif core == hs:
+                g.wait_ge(sem.arr_hs, _engines(src, core, topo)[1])
+                n = send(dst, T.r_bs[:, 0:NC], T.h_s[:, 0:NC], sem.arr_bs)
+                g.wait_ge(sem.out, n)
+        return
+
+    row, col = divmod(rank, GR)
+    peer_a = cores[GR * row + (1 - col)]
+    peer_b = partner_b[core]
+    hc, hs = _helpers(core, peer_b, topo)
+    in_hc, in_hs = _helpers(peer_b, core, topo)
+
+    for t, tx, tw, x, w in (("b", T.t_xb, T.t_wb, T.xb, T.wb), ("a", T.t_xa, T.t_wa, T.xa, T.wa)):
+        g.sync.dma_start(tx[:, 0:TW], x[:, 0:TW]).then_inc(sem["l_x" + t], 16)
+        g.scalar.dma_start(tw[:, 0:TW], w[:, 0:TW]).then_inc(sem["l_w0" + t], 16)
+        g.sync.dma_start(tw[:, TW:2 * TW], w[:, TW:2 * TW]).then_inc(sem["l_w1" + t], 16)
+
+    for t in ("b", "a"):
+        tx, tw, tt = T["t_x" + t], T["t_w" + t], T["t_" + t]
+        cx, sx, cw, sw, ct, st = (T["c_x" + t], T["s_x" + t], T["c_w" + t], T["s_w" + t], T["c_" + t], T["s_" + t])
+        z = (T["z" + t + "0"], T["z" + t + "1"])
+        v, pe, ac = g.vector, g.tensor, g.scalar
+        v.wait_ge(sem["l_x" + t], 16)
+        v.quantize_mx(cx[:, 0:NC], sx[:, 0:NC], tx[:, 0:TW]).then_inc(sem["q_x" + t], 1)
+        for i in range(2):
+            v.wait_ge(sem["l_w%d" % i + t], 16)
+            v.quantize_mx(cw[:, NC * i:NC * (i + 1)], sw[:, NC * i:NC * (i + 1)],
+                          tw[:, TW * i:TW * (i + 1)]).then_inc(sem["q_w%d" % i + t], 1)
+        pe.wait_ge(sem["q_x" + t], 1)
+        for i in range(2):
+            pe.wait_ge(sem["q_w%d" % i + t], 1)
+            pe.matmul_mx(z[i][:, 0:NC], cw[:, NC * i:NC * (i + 1)], sw[:, NC * i:NC * (i + 1)],
+                         cx[:, 0:NC], sx[:, 0:NC], True, True).then_inc(sem["m%d" % i + t], 1)
+        ac.wait_ge(sem["m0" + t], 1)
+        for b, s in ((0, SCALE), (1, -SCALE)):
+            ac.activation(tt[:, b:TW:4], z[0][:, 0:NC], ActivationFunctionType.Relu, scale=s).then_inc(sem["act" + t], 1)
+        v.wait_ge(sem["m1" + t], 1)
+        for b, s in ((2, SCALE), (3, -SCALE)):
+            v.tensor_scalar(tt[:, b:TW:4], z[1][:, 0:NC], s, 0.0, AluOpType.mult, AluOpType.max).then_inc(sem["vec" + t], 1)
+        v.wait_ge(sem["vec" + t], 2)
+        v.wait_ge(sem["act" + t], 2)
+        v.quantize_mx(ct[:, 0:NC], st[:, 0:NC], tt[:, 0:TW]).then_inc(sem["q_t" + t], 1)
+
+    sent = 0
+    g.wait_ge(sem.q_tb, 1)
+    sent += send(hc, T.h_c[:, 0:NC].bitcast(u8), T.c_b[:, 0:NC].bitcast(u8), sem.arr_hc)
+    sent += send(hs, T.h_s[:, 0:NC], T.s_b[:, 0:NC], sem.arr_hs)
+    g.wait_ge(sem.q_ta, 1)
+    sent += send(peer_a, T.r_ac[:, 0:NC].bitcast(u8), T.c_a[:, 0:NC].bitcast(u8), sem.arr_ac)
+    sent += send(peer_a, T.r_as[:, 0:NC], T.s_a[:, 0:NC], sem.arr_as)
+    g.wait_ge(sem.out, sent)
+
+    pe = g.tensor
+    pe.wait_ge(sem.q_tb, 1)
+    pe.wait_ge(sem.q_ta, 1)
+
+    def a_side(k):
+        if k == col:
+            return T.c_a, T.s_a
+        pe.wait_ge(sem.arr_ac, _engines(peer_a, core, topo)[1])
+        pe.wait_ge(sem.arr_as, _engines(peer_a, core, topo)[1])
+        return T.r_ac, T.r_as
+
+    lc, ls = a_side(row)
+    pe.matmul_mx(T.zy[:, 0:NC], lc[:, 0:NC], ls[:, 0:NC], T.c_b[:, 0:NC], T.s_b[:, 0:NC], True, False)
+    lc, ls = a_side(1 - row)
+    pe.wait_ge(sem.arr_bs, _engines(in_hs, core, topo)[1])
+    pe.wait_ge(sem.arr_bc, _engines(in_hc, core, topo)[1])
+    pe.matmul_mx(T.zy[:, 0:NC], lc[:, 0:NC], ls[:, 0:NC], T.r_bc[:, 0:NC], T.r_bs[:, 0:NC], False, True).then_inc(sem.y_mm, 1)
+    g.vector.wait_ge(sem.y_mm, 1)
+    g.vector.tensor_copy(T.o[:, 0:NC], T.zy[:, 0:NC]).then_inc(sem.fin, 1)
+    g.sync.wait_ge(sem.fin, 1)
+    g.sync.dma_start(T.y[:, 0:NC], T.o[:, 0:NC]).then_inc(sem.stored, 16)
+    g.sync.wait_ge(sem.stored, 16)

@@ -1,6 +1,8 @@
+from concourse.bass import DstId, RemoteDMATransfer
 from concourse.mybir import dt, AluOpType, ActivationFunctionType
 
 NC = 128
+HC = NC // 2
 TW = 4 * NC
 GR = 2
 SCALE = 0.029
@@ -24,7 +26,7 @@ SCRATCH = {
     "za0": ("psum", [128, 512], "float32"), "za1": ("psum", [128, 512], "float32"),
     "zy": ("psum", [128, 512], "float32"),
 }
-SEMAPHORES = ["out", "arr_hc", "arr_hs", "arr_ac", "arr_as", "arr_bc", "arr_bs", "fin", "stored", "y_mm"]
+SEMAPHORES = ["out", "arr_h", "arr_ac", "arr_as", "arr_b0", "arr_b1", "arr_bs", "fin", "stored", "y_mm"]
 for _t in ("a", "b"):
     SEMAPHORES += [_n + _t for _n in ("l_x", "l_w0", "l_w1", "q_x", "q_w0", "q_w1", "m0", "m1", "act", "vec", "q_t")]
 
@@ -36,12 +38,11 @@ def _helpers(src, dst, topo):
             and topo.may_write(src, c) and topo.may_write(c, dst) and topo.host(c) not in (host, topo.host(dst))]
     far = [c for c in free if topo.rack(topo.host(c)) != topo.rack(host)]
     near = [c for c in free if topo.rack(topo.host(c)) == topo.rack(host)]
-    return far[0], near[-1]
+    return far[0], near[-1], near[-3]
 
 
-def _engines(src, dst, topo):
-    bits = [e for e in range(16) if topo.mask(src, dst) >> e & 1]
-    return sum(1 << e for e in bits[::2]), len(bits[::2])
+def _bits(src, dst, topo):
+    return [e for e in range(16) if topo.mask(src, dst) >> e & 1]
 
 
 def rank_program(g, core, T, topo):
@@ -51,32 +52,38 @@ def rank_program(g, core, T, topo):
     sem = T.sem
     u8 = dt.uint8
 
-    def send(dst, out_ap, in_ap, remote_sem):
+    def send(dst, out_ap, in_ap, remote_sem, bits):
         rid, pid = topo.addr(dst, core)
-        m, n = _engines(core, dst, topo)
         g.remote_dma(out_ap=out_ap, in_ap=in_ap, remote_sem=remote_sem, local_sem=sem.out, pid=pid, routing_id=rid,
-                     dma_engine_mask=m)
-        return n
+                     dma_engine_mask=sum(1 << e for e in bits))
+        return len(bits)
+
+    def half(buf, i):
+        return buf[:, HC * i:HC * (i + 1)].bitcast(u8)
 
     if rank is None:
         for src in cores:
             dst = partner_b[src]
-            hc, hs = _helpers(src, dst, topo)
-            if core == hc:
-                g.wait_ge(sem.arr_hc, _engines(src, core, topo)[1])
-                n = send(dst, T.r_bc[:, 0:NC].bitcast(u8), T.h_c[:, 0:NC].bitcast(u8), sem.arr_bc)
-                g.wait_ge(sem.out, n)
-            elif core == hs:
-                g.wait_ge(sem.arr_hs, _engines(src, core, topo)[1])
-                n = send(dst, T.r_bs[:, 0:NC], T.h_s[:, 0:NC], sem.arr_bs)
-                g.wait_ge(sem.out, n)
+            if topo.chip(core) != topo.chip(src):
+                continue
+            hs = _helpers(src, dst, topo)
+            if core not in hs:
+                continue
+            i = hs.index(core)
+            g.wait_ge(sem.arr_h, len(_bits(src, core, topo)) // (2 if i < 2 else 1))
+            bits = _bits(core, dst, topo)[::2]
+            if i < 2:
+                n = send(dst, half(T.r_bc, i), half(T.h_c, i), sem["arr_b%d" % i], bits)
+            else:
+                n = send(dst, T.r_bs[:, 0:NC], T.h_s[:, 0:NC], sem.arr_bs, bits)
+            g.wait_ge(sem.out, n)
         return
 
     row, col = divmod(rank, GR)
     peer_a = cores[GR * row + (1 - col)]
     peer_b = partner_b[core]
-    hc, hs = _helpers(core, peer_b, topo)
-    in_hc, in_hs = _helpers(peer_b, core, topo)
+    hs = _helpers(core, peer_b, topo)
+    in_hs = _helpers(peer_b, core, topo)
 
     for t, tx, tw, x, w in (("b", T.t_xb, T.t_wb, T.xb, T.wb), ("a", T.t_xa, T.t_wa, T.xa, T.wa)):
         g.sync.dma_start(tx[:, 0:TW], x[:, 0:TW]).then_inc(sem["l_x" + t], 16)
@@ -111,11 +118,18 @@ def rank_program(g, core, T, topo):
 
     sent = 0
     g.wait_ge(sem.q_tb, 1)
-    sent += send(hc, T.h_c[:, 0:NC].bitcast(u8), T.c_b[:, 0:NC].bitcast(u8), sem.arr_hc)
-    sent += send(hs, T.h_s[:, 0:NC], T.s_b[:, 0:NC], sem.arr_hs)
+    transfers = []
+    for i in range(2):
+        rid, pid = topo.addr(hs[i], core)
+        bits = _bits(core, hs[i], topo)[i::2]
+        transfers.append(RemoteDMATransfer(dst_ids=[DstId(rid=rid, pnc=pid)], dma_engine_mask=sum(1 << e for e in bits),
+                                           remote_sem=sem.arr_h, srcs=[half(T.c_b, i)], dsts=[half(T.h_c, i)]))
+        sent += len(bits)
+    g.remote_dma_fused(transfers, local_sem=sem.out)
+    sent += send(hs[2], T.h_s[:, 0:NC], T.s_b[:, 0:NC], sem.arr_h, _bits(core, hs[2], topo))
     g.wait_ge(sem.q_ta, 1)
-    sent += send(peer_a, T.r_ac[:, 0:NC].bitcast(u8), T.c_a[:, 0:NC].bitcast(u8), sem.arr_ac)
-    sent += send(peer_a, T.r_as[:, 0:NC], T.s_a[:, 0:NC], sem.arr_as)
+    sent += send(peer_a, T.r_ac[:, 0:NC].bitcast(u8), T.c_a[:, 0:NC].bitcast(u8), sem.arr_ac, _bits(core, peer_a, topo))
+    sent += send(peer_a, T.r_as[:, 0:NC], T.s_a[:, 0:NC], sem.arr_as, _bits(core, peer_a, topo))
     g.wait_ge(sem.out, sent)
 
     pe = g.tensor
@@ -125,15 +139,15 @@ def rank_program(g, core, T, topo):
     def a_side(k):
         if k == col:
             return T.c_a, T.s_a
-        pe.wait_ge(sem.arr_ac, _engines(peer_a, core, topo)[1])
-        pe.wait_ge(sem.arr_as, _engines(peer_a, core, topo)[1])
+        pe.wait_ge(sem.arr_ac, len(_bits(peer_a, core, topo)))
+        pe.wait_ge(sem.arr_as, len(_bits(peer_a, core, topo)))
         return T.r_ac, T.r_as
 
     lc, ls = a_side(row)
     pe.matmul_mx(T.zy[:, 0:NC], lc[:, 0:NC], ls[:, 0:NC], T.c_b[:, 0:NC], T.s_b[:, 0:NC], True, False)
     lc, ls = a_side(1 - row)
-    pe.wait_ge(sem.arr_bs, _engines(in_hs, core, topo)[1])
-    pe.wait_ge(sem.arr_bc, _engines(in_hc, core, topo)[1])
+    for name, h in (("arr_bs", in_hs[2]), ("arr_b0", in_hs[0]), ("arr_b1", in_hs[1])):
+        pe.wait_ge(sem[name], len(_bits(h, core, topo)[::2]))
     pe.matmul_mx(T.zy[:, 0:NC], lc[:, 0:NC], ls[:, 0:NC], T.r_bc[:, 0:NC], T.r_bs[:, 0:NC], False, True).then_inc(sem.y_mm, 1)
     g.vector.wait_ge(sem.y_mm, 1)
     g.vector.tensor_copy(T.o[:, 0:NC], T.zy[:, 0:NC]).then_inc(sem.fin, 1)

@@ -2,10 +2,11 @@ from concourse.bass import DstId, RemoteDMATransfer
 from concourse.mybir import dt, AluOpType, ActivationFunctionType
 
 NC = 128
-HC = NC // 2
 TW = 4 * NC
 GR = 2
 SCALE = 0.029
+PC = NC // 4
+CUT = ((0, (NC - PC) // 2), ((NC - PC) // 2, NC - PC), (NC - PC, NC))
 
 _C, _S = "float8_e4m3fn_x4", "uint8"
 SCRATCH = {
@@ -20,13 +21,13 @@ SCRATCH = {
     "c_b": ("sbuf", [128, NC], _C), "s_b": ("sbuf", [128, NC], _S),
     "r_ac": ("sbuf", [128, NC], _C), "r_as": ("sbuf", [128, NC], _S),
     "r_bc": ("sbuf", [128, NC], _C), "r_bs": ("sbuf", [128, NC], _S),
-    "h_c": ("sbuf", [128, NC], _C), "h_s": ("sbuf", [128, NC], _S),
+    "f_c": ("sbuf", [128, NC], _C), "f_s": ("sbuf", [128, NC], _S),
     "o": ("sbuf", [128, NC], "float32"),
     "zb0": ("psum", [128, 512], "float32"), "zb1": ("psum", [128, 512], "float32"),
     "za0": ("psum", [128, 512], "float32"), "za1": ("psum", [128, 512], "float32"),
     "zy": ("psum", [128, 512], "float32"),
 }
-SEMAPHORES = ["out", "arr_h", "arr_ac", "arr_as", "arr_b0", "arr_b1", "arr_bs", "fin", "stored", "y_mm"]
+SEMAPHORES = ["out", "arr_f", "arr_ac", "arr_as", "arr_b0", "arr_b1", "arr_bf", "fin", "stored", "y_mm"]
 for _t in ("a", "b"):
     SEMAPHORES += [_n + _t for _n in ("l_x", "l_w0", "l_w1", "q_x", "q_w0", "q_w1", "m0", "m1", "act", "vec", "q_t")]
 
@@ -38,7 +39,7 @@ def _helpers(src, dst, topo):
             and topo.may_write(src, c) and topo.may_write(c, dst) and topo.host(c) not in (host, topo.host(dst))]
     far = [c for c in free if topo.rack(topo.host(c)) != topo.rack(host)]
     near = [c for c in free if topo.rack(topo.host(c)) == topo.rack(host)]
-    return far[0], near[-1], near[-3]
+    return far[0], near[-1]
 
 
 def _bits(src, dst, topo):
@@ -52,14 +53,28 @@ def rank_program(g, core, T, topo):
     sem = T.sem
     u8 = dt.uint8
 
+    def mask(bits):
+        return sum(1 << e for e in bits)
+
     def send(dst, out_ap, in_ap, remote_sem, bits):
         rid, pid = topo.addr(dst, core)
         g.remote_dma(out_ap=out_ap, in_ap=in_ap, remote_sem=remote_sem, local_sem=sem.out, pid=pid, routing_id=rid,
-                     dma_engine_mask=sum(1 << e for e in bits))
+                     dma_engine_mask=mask(bits))
         return len(bits)
 
-    def half(buf, i):
-        return buf[:, HC * i:HC * (i + 1)].bitcast(u8)
+    def send_two(pairs):
+        transfers, n = [], 0
+        for i, (dst, out_ap, in_ap, remote_sem) in enumerate(pairs):
+            rid, pid = topo.addr(dst, core)
+            bits = _bits(core, dst, topo)[i::2]
+            transfers.append(RemoteDMATransfer(dst_ids=[DstId(rid=rid, pnc=pid)], dma_engine_mask=mask(bits),
+                                               remote_sem=remote_sem, srcs=[in_ap], dsts=[out_ap]))
+            n += len(bits)
+        g.remote_dma_fused(transfers, local_sem=sem.out)
+        return n
+
+    def piece(buf, i):
+        return buf[:, CUT[i][0]:CUT[i][1]].bitcast(u8)
 
     if rank is None:
         for src in cores:
@@ -70,25 +85,26 @@ def rank_program(g, core, T, topo):
             if core not in hs:
                 continue
             i = hs.index(core)
-            g.wait_ge(sem.arr_h, len(_bits(src, core, topo)) // (2 if i < 2 else 1))
-            bits = _bits(core, dst, topo)[::2]
-            if i < 2:
-                n = send(dst, half(T.r_bc, i), half(T.h_c, i), sem["arr_b%d" % i], bits)
-            else:
-                n = send(dst, T.r_bs[:, 0:NC], T.h_s[:, 0:NC], sem.arr_bs, bits)
+            g.wait_ge(sem.arr_f, len(_bits(src, core, topo)[i::2]))
+            n = send(dst, piece(T.r_bc, i), piece(T.f_c, i), sem["arr_b%d" % i], _bits(core, dst, topo)[::2])
             g.wait_ge(sem.out, n)
         return
 
     row, col = divmod(rank, GR)
     peer_a = cores[GR * row + (1 - col)]
     peer_b = partner_b[core]
+    cabled = partner_b[peer_a]
     hs = _helpers(core, peer_b, topo)
     in_hs = _helpers(peer_b, core, topo)
+    n_in = {c: [len(_bits(c, core, topo)[i::2]) for i in range(2)] for c in (peer_a, cabled)}
 
-    for t, tx, tw, x, w in (("b", T.t_xb, T.t_wb, T.xb, T.wb), ("a", T.t_xa, T.t_wa, T.xa, T.wa)):
-        g.sync.dma_start(tx[:, 0:TW], x[:, 0:TW]).then_inc(sem["l_x" + t], 16)
-        g.scalar.dma_start(tw[:, 0:TW], w[:, 0:TW]).then_inc(sem["l_w0" + t], 16)
-        g.sync.dma_start(tw[:, TW:2 * TW], w[:, TW:2 * TW]).then_inc(sem["l_w1" + t], 16)
+    g.scalar.dma_start(T.t_wb[:, 0:TW], T.wb[:, 0:TW]).then_inc(sem.l_w0b, 16)
+    g.sync.dma_start(T.t_xb[:, 0:TW], T.xb[:, 0:TW]).then_inc(sem.l_xb, 16)
+    g.sync.dma_start(T.t_wb[:, TW:2 * TW], T.wb[:, TW:2 * TW]).then_inc(sem.l_w1b, 16)
+    g.sync.wait_ge(sem.l_xb, 16)
+    g.sync.dma_start(T.t_xa[:, 0:TW], T.xa[:, 0:TW]).then_inc(sem.l_xa, 16)
+    for i in range(2):
+        g.sync.dma_start(T.t_wa[:, TW * i:TW * (i + 1)], T.wa[:, TW * i:TW * (i + 1)]).then_inc(sem["l_w%da" % i], 16)
 
     for t in ("b", "a"):
         tx, tw, tt = T["t_x" + t], T["t_w" + t], T["t_" + t]
@@ -116,20 +132,16 @@ def rank_program(g, core, T, topo):
         v.wait_ge(sem["act" + t], 2)
         v.quantize_mx(ct[:, 0:NC], st[:, 0:NC], tt[:, 0:TW]).then_inc(sem["q_t" + t], 1)
 
-    sent = 0
     g.wait_ge(sem.q_tb, 1)
-    transfers = []
-    for i in range(2):
-        rid, pid = topo.addr(hs[i], core)
-        bits = _bits(core, hs[i], topo)[i::2]
-        transfers.append(RemoteDMATransfer(dst_ids=[DstId(rid=rid, pnc=pid)], dma_engine_mask=sum(1 << e for e in bits),
-                                           remote_sem=sem.arr_h, srcs=[half(T.c_b, i)], dsts=[half(T.h_c, i)]))
-        sent += len(bits)
-    g.remote_dma_fused(transfers, local_sem=sem.out)
-    sent += send(hs[2], T.h_s[:, 0:NC], T.s_b[:, 0:NC], sem.arr_h, _bits(core, hs[2], topo))
+    sent = send_two([(hs[i], piece(T.f_c, i), piece(T.c_b, i), sem.arr_f) for i in range(2)])
+    sent += send_two([(cabled, piece(T.f_c, 2), piece(T.c_b, 2), sem.arr_f),
+                      (peer_a, T.f_s[:, 0:NC], T.s_b[:, 0:NC], sem.arr_f)])
     g.wait_ge(sem.q_ta, 1)
     sent += send(peer_a, T.r_ac[:, 0:NC].bitcast(u8), T.c_a[:, 0:NC].bitcast(u8), sem.arr_ac, _bits(core, peer_a, topo))
     sent += send(peer_a, T.r_as[:, 0:NC], T.s_a[:, 0:NC], sem.arr_as, _bits(core, peer_a, topo))
+    g.wait_ge(sem.arr_f, n_in[cabled][0] + n_in[peer_a][1])
+    sent += send_two([(peer_a, piece(T.r_bc, 2), piece(T.f_c, 2), sem.arr_bf),
+                      (cabled, T.r_bs[:, 0:NC], T.f_s[:, 0:NC], sem.arr_bf)])
     g.wait_ge(sem.out, sent)
 
     pe = g.tensor
@@ -146,8 +158,9 @@ def rank_program(g, core, T, topo):
     lc, ls = a_side(row)
     pe.matmul_mx(T.zy[:, 0:NC], lc[:, 0:NC], ls[:, 0:NC], T.c_b[:, 0:NC], T.s_b[:, 0:NC], True, False)
     lc, ls = a_side(1 - row)
-    for name, h in (("arr_bs", in_hs[2]), ("arr_b0", in_hs[0]), ("arr_b1", in_hs[1])):
-        pe.wait_ge(sem[name], len(_bits(h, core, topo)[::2]))
+    pe.wait_ge(sem.arr_bf, n_in[peer_a][0] + n_in[cabled][1])
+    for i in range(2):
+        pe.wait_ge(sem["arr_b%d" % i], len(_bits(in_hs[i], core, topo)[::2]))
     pe.matmul_mx(T.zy[:, 0:NC], lc[:, 0:NC], ls[:, 0:NC], T.r_bc[:, 0:NC], T.r_bs[:, 0:NC], False, True).then_inc(sem.y_mm, 1)
     g.vector.wait_ge(sem.y_mm, 1)
     g.vector.tensor_copy(T.o[:, 0:NC], T.zy[:, 0:NC]).then_inc(sem.fin, 1)

from concourse.bass import DstId, RemoteDMATransfer
from concourse.mybir import dt, AluOpType, ActivationFunctionType

NC = 128
TW = 4 * NC
GR = 2
SCALE = 0.029
PC = NC // 4
CUT = ((0, (NC - PC) // 2), ((NC - PC) // 2, NC - PC), (NC - PC, NC))

_C, _S = "float8_e4m3fn_x4", "uint8"
SCRATCH = {
    "t_xb": ("sbuf", [128, TW], "bfloat16"), "t_wb": ("sbuf", [128, 2 * TW], "bfloat16"),
    "t_xa": ("sbuf", [128, TW], "bfloat16"), "t_wa": ("sbuf", [128, 2 * TW], "bfloat16"),
    "t_a": ("sbuf", [128, TW], "bfloat16"), "t_b": ("sbuf", [128, TW], "bfloat16"),
    "c_xb": ("sbuf", [128, NC], _C), "s_xb": ("sbuf", [128, NC], _S),
    "c_wb": ("sbuf", [128, 2 * NC], _C), "s_wb": ("sbuf", [128, 2 * NC], _S),
    "c_xa": ("sbuf", [128, NC], _C), "s_xa": ("sbuf", [128, NC], _S),
    "c_wa": ("sbuf", [128, 2 * NC], _C), "s_wa": ("sbuf", [128, 2 * NC], _S),
    "c_a": ("sbuf", [128, NC], _C), "s_a": ("sbuf", [128, NC], _S),
    "c_b": ("sbuf", [128, NC], _C), "s_b": ("sbuf", [128, NC], _S),
    "r_ac": ("sbuf", [128, NC], _C), "r_as": ("sbuf", [128, NC], _S),
    "r_bc": ("sbuf", [128, NC], _C), "r_bs": ("sbuf", [128, NC], _S),
    "f_c": ("sbuf", [128, NC], _C), "f_s": ("sbuf", [128, NC], _S),
    "o": ("sbuf", [128, NC], "float32"),
    "zb0": ("psum", [128, 512], "float32"), "zb1": ("psum", [128, 512], "float32"),
    "za0": ("psum", [128, 512], "float32"), "za1": ("psum", [128, 512], "float32"),
    "zy": ("psum", [128, 512], "float32"),
}
SEMAPHORES = ["out", "arr_f", "arr_ac", "arr_as", "arr_b0", "arr_b1", "arr_bf", "fin", "stored", "y_mm"]
for _t in ("a", "b"):
    SEMAPHORES += [_n + _t for _n in ("l_x", "l_w0", "l_w1", "q_x", "q_w0", "q_w1", "m0", "m1", "act", "vec", "q_t")]


def _helpers(src, dst, topo):
    host = topo.host(src)
    free = [c for c in range(512)
            if topo.chip(c) == topo.chip(src) and topo.die(c) != topo.die(src)
            and topo.may_write(src, c) and topo.may_write(c, dst) and topo.host(c) not in (host, topo.host(dst))]
    far = [c for c in free if topo.rack(topo.host(c)) != topo.rack(host)]
    near = [c for c in free if topo.rack(topo.host(c)) == topo.rack(host)]
    return far[0], near[-1]


def _bits(src, dst, topo):
    return [e for e in range(16) if topo.mask(src, dst) >> e & 1]


def rank_program(g, core, T, topo):
    cores = list(T.cores)
    partner_b = {c: cores[(r + GR) % len(cores)] for r, c in enumerate(cores)}
    rank = T.rank_of(core)
    sem = T.sem
    u8 = dt.uint8

    def mask(bits):
        return sum(1 << e for e in bits)

    def send(dst, out_ap, in_ap, remote_sem, bits):
        rid, pid = topo.addr(dst, core)
        g.remote_dma(out_ap=out_ap, in_ap=in_ap, remote_sem=remote_sem, local_sem=sem.out, pid=pid, routing_id=rid,
                     dma_engine_mask=mask(bits))
        return len(bits)

    def send_two(pairs):
        transfers, n = [], 0
        for i, (dst, out_ap, in_ap, remote_sem) in enumerate(pairs):
            rid, pid = topo.addr(dst, core)
            bits = _bits(core, dst, topo)[i::2]
            transfers.append(RemoteDMATransfer(dst_ids=[DstId(rid=rid, pnc=pid)], dma_engine_mask=mask(bits),
                                               remote_sem=remote_sem, srcs=[in_ap], dsts=[out_ap]))
            n += len(bits)
        g.remote_dma_fused(transfers, local_sem=sem.out)
        return n

    def piece(buf, i):
        return buf[:, CUT[i][0]:CUT[i][1]].bitcast(u8)

    if rank is None:
        for src in cores:
            dst = partner_b[src]
            if topo.chip(core) != topo.chip(src):
                continue
            hs = _helpers(src, dst, topo)
            if core not in hs:
                continue
            i = hs.index(core)
            g.wait_ge(sem.arr_f, len(_bits(src, core, topo)[i::2]))
            n = send(dst, piece(T.r_bc, i), piece(T.f_c, i), sem["arr_b%d" % i], _bits(core, dst, topo)[::2])
            g.wait_ge(sem.out, n)
        return

    row, col = divmod(rank, GR)
    peer_a = cores[GR * row + (1 - col)]
    peer_b = partner_b[core]
    cabled = partner_b[peer_a]
    hs = _helpers(core, peer_b, topo)
    in_hs = _helpers(peer_b, core, topo)
    n_in = {c: [len(_bits(c, core, topo)[i::2]) for i in range(2)] for c in (peer_a, cabled)}

    g.scalar.dma_start(T.t_wb[:, 0:TW], T.wb[:, 0:TW]).then_inc(sem.l_w0b, 16)
    g.sync.dma_start(T.t_xb[:, 0:TW], T.xb[:, 0:TW]).then_inc(sem.l_xb, 16)
    g.sync.dma_start(T.t_wb[:, TW:2 * TW], T.wb[:, TW:2 * TW]).then_inc(sem.l_w1b, 16)
    g.sync.wait_ge(sem.l_xb, 16)
    g.sync.dma_start(T.t_xa[:, 0:TW], T.xa[:, 0:TW]).then_inc(sem.l_xa, 16)
    for i in range(2):
        g.sync.dma_start(T.t_wa[:, TW * i:TW * (i + 1)], T.wa[:, TW * i:TW * (i + 1)]).then_inc(sem["l_w%da" % i], 16)

    for t in ("b", "a"):
        tx, tw, tt = T["t_x" + t], T["t_w" + t], T["t_" + t]
        cx, sx, cw, sw, ct, st = (T["c_x" + t], T["s_x" + t], T["c_w" + t], T["s_w" + t], T["c_" + t], T["s_" + t])
        z = (T["z" + t + "0"], T["z" + t + "1"])
        v, pe, ac = g.vector, g.tensor, g.scalar
        v.wait_ge(sem["l_x" + t], 16)
        v.quantize_mx(cx[:, 0:NC], sx[:, 0:NC], tx[:, 0:TW]).then_inc(sem["q_x" + t], 1)
        for i in range(2):
            v.wait_ge(sem["l_w%d" % i + t], 16)
            v.quantize_mx(cw[:, NC * i:NC * (i + 1)], sw[:, NC * i:NC * (i + 1)],
                          tw[:, TW * i:TW * (i + 1)]).then_inc(sem["q_w%d" % i + t], 1)
        pe.wait_ge(sem["q_x" + t], 1)
        for i in range(2):
            pe.wait_ge(sem["q_w%d" % i + t], 1)
            pe.matmul_mx(z[i][:, 0:NC], cw[:, NC * i:NC * (i + 1)], sw[:, NC * i:NC * (i + 1)],
                         cx[:, 0:NC], sx[:, 0:NC], True, True).then_inc(sem["m%d" % i + t], 1)
        ac.wait_ge(sem["m0" + t], 1)
        for b, s in ((0, SCALE), (1, -SCALE)):
            ac.activation(tt[:, b:TW:4], z[0][:, 0:NC], ActivationFunctionType.Relu, scale=s).then_inc(sem["act" + t], 1)
        v.wait_ge(sem["m1" + t], 1)
        for b, s in ((2, SCALE), (3, -SCALE)):
            v.tensor_scalar(tt[:, b:TW:4], z[1][:, 0:NC], s, 0.0, AluOpType.mult, AluOpType.max).then_inc(sem["vec" + t], 1)
        v.wait_ge(sem["vec" + t], 2)
        v.wait_ge(sem["act" + t], 2)
        v.quantize_mx(ct[:, 0:NC], st[:, 0:NC], tt[:, 0:TW]).then_inc(sem["q_t" + t], 1)

    g.wait_ge(sem.q_tb, 1)
    sent = send_two([(hs[i], piece(T.f_c, i), piece(T.c_b, i), sem.arr_f) for i in range(2)])
    sent += send_two([(cabled, piece(T.f_c, 2), piece(T.c_b, 2), sem.arr_f),
                      (peer_a, T.f_s[:, 0:NC], T.s_b[:, 0:NC], sem.arr_f)])
    g.wait_ge(sem.q_ta, 1)
    sent += send(peer_a, T.r_ac[:, 0:NC].bitcast(u8), T.c_a[:, 0:NC].bitcast(u8), sem.arr_ac, _bits(core, peer_a, topo))
    sent += send(peer_a, T.r_as[:, 0:NC], T.s_a[:, 0:NC], sem.arr_as, _bits(core, peer_a, topo))
    g.wait_ge(sem.arr_f, n_in[cabled][0] + n_in[peer_a][1])
    sent += send_two([(peer_a, piece(T.r_bc, 2), piece(T.f_c, 2), sem.arr_bf),
                      (cabled, T.r_bs[:, 0:NC], T.f_s[:, 0:NC], sem.arr_bf)])
    g.wait_ge(sem.out, sent)

    pe = g.tensor
    pe.wait_ge(sem.q_tb, 1)
    pe.wait_ge(sem.q_ta, 1)

    def a_side(k):
        if k == col:
            return T.c_a, T.s_a
        pe.wait_ge(sem.arr_ac, len(_bits(peer_a, core, topo)))
        pe.wait_ge(sem.arr_as, len(_bits(peer_a, core, topo)))
        return T.r_ac, T.r_as

    lc, ls = a_side(row)
    pe.matmul_mx(T.zy[:, 0:NC], lc[:, 0:NC], ls[:, 0:NC], T.c_b[:, 0:NC], T.s_b[:, 0:NC], True, False)
    lc, ls = a_side(1 - row)
    pe.wait_ge(sem.arr_bf, n_in[peer_a][0] + n_in[cabled][1])
    for i in range(2):
        pe.wait_ge(sem["arr_b%d" % i], len(_bits(in_hs[i], core, topo)[::2]))
    pe.matmul_mx(T.zy[:, 0:NC], lc[:, 0:NC], ls[:, 0:NC], T.r_bc[:, 0:NC], T.r_bs[:, 0:NC], False, True).then_inc(sem.y_mm, 1)
    g.vector.wait_ge(sem.y_mm, 1)
    g.vector.tensor_copy(T.o[:, 0:NC], T.zy[:, 0:NC]).then_inc(sem.fin, 1)
    g.sync.wait_ge(sem.fin, 1)
    g.sync.dma_start(T.y[:, 0:NC], T.o[:, 0:NC]).then_inc(sem.stored, 16)
    g.sync.wait_ge(sem.stored, 16)
